import numpy as np
import ml_dtypes


def mxq(x, axis, fmt="e4m3"):
    dtype, down = {"e4m3": (ml_dtypes.float8_e4m3fn, 7), "e5m2": (ml_dtypes.float8_e5m2, 14)}[fmt]
    v = np.moveaxis(np.asarray(x, np.float32).astype(ml_dtypes.bfloat16).astype(np.float64), axis, -1)
    blocks = v.reshape(v.shape[:-1] + (-1, 32))
    amax = np.abs(blocks).max(-1, keepdims=True)
    byte = np.maximum(np.where(amax > 0, np.frexp(amax)[1] - 1 + 127, 0) - down, 1)
    scale = np.exp2(byte - 127.0)
    codes = (blocks / scale).astype(np.float32).astype(dtype).astype(np.float64)
    return np.moveaxis((codes * scale).reshape(v.shape), -1, axis)


WIDE = False


def mx_kscale(k):
    if not WIDE:
        return np.ones(k)
    levels = np.array([10, -10, 5, -5, 0])
    if k % 512:
        return np.exp2(np.random.permutation(np.resize(levels, k // 32))).repeat(32)
    a = np.empty((k // 512, 16))
    for p in range(k // 512):
        a[p, :8] = np.random.permutation(np.resize(levels, 8))
        for g in range(8):
            far = levels[np.abs(levels - a[p, g]) >= 10]
            a[p, g + 8] = far[np.random.randint(len(far))]
    return np.exp2(a.ravel()).repeat(32)


def f64(x):
    return np.asarray(x).astype(np.float64)


def striped(idx):
    return np.tile(np.asarray(idx).reshape(-1, 16).T, (8, 1)).astype(np.uint16)


def unstriped(offs):
    return offs[:16].T.reshape(-1).astype(np.int64)


E2M1 = np.array([0.0, 0.5, 1.0, 1.5, 2.0, 3.0, 4.0, 6.0, -0.0, -0.5, -1.0, -1.5, -2.0, -3.0, -4.0, -6.0])


def pack_weight(w, fmt):
    k, n = w.shape
    w = f64(np.asarray(w, np.float32).astype(ml_dtypes.bfloat16)).reshape(k // 32, 32, n)
    amax = np.abs(w).max(1)
    if fmt == "e4m3":
        byte = np.frexp(amax)[1] - 1 + 127 - 7
    else:
        mant, ex = np.frexp(amax / 6.0)
        byte = np.where(mant > 0.5, ex, ex - 1) + 127
    byte = np.clip(np.where(amax > 0, byte, 1), 1, 254)
    scaled = (w * np.exp2(127.0 - byte)[:, None, :]).reshape(k, n).astype(np.float32)
    by_word = np.ascontiguousarray(scaled.reshape(k // 512, 128, 4, n).transpose(0, 1, 3, 2))
    if fmt == "e4m3":
        words = by_word.astype(ml_dtypes.float8_e4m3fn).view(np.uint8)
    else:
        c = by_word.astype(ml_dtypes.float4_e2m1fn).view(np.uint8) & 0xF
        words = (c[..., 0::2] | (c[..., 1::2] << 4)).reshape(k // 512, 128, 2 * n)
    return np.ascontiguousarray(words), np.ascontiguousarray(byte.astype(np.uint8).reshape(k // 512, 16, n))


def unpack_weight(words, scales, fmt):
    g, _, n = scales.shape
    words = np.ascontiguousarray(words).reshape(g, 128, n, -1)
    if fmt == "e4m3":
        vals = words.view(ml_dtypes.float8_e4m3fn).astype(np.float64)
    else:
        nib = np.empty((g, 128, n, 4), np.uint8)
        nib[..., 0::2] = words & 0xF
        nib[..., 1::2] = words >> 4
        vals = E2M1[nib]
    vals = vals * np.repeat(np.exp2(scales.astype(np.float64) - 127.0), 8, axis=1)[..., None]
    return vals.transpose(0, 1, 3, 2).reshape(g * 512, n)


D, T, I, J, U, Z, E = 512, 2048, 512, 512, 1024, 1024, 512


def setup_inputs():
    n = np.random.standard_normal
    idx = np.random.permutation(T)[:I]
    idx2 = np.random.permutation(U)[:J]
    idx3 = np.random.permutation(Z)[:J]
    fd = mx_kscale(D)
    fi = mx_kscale(I)
    ti = np.ones(T)
    ti[idx] = fi
    keysp = pack_weight(n((D, T)) / fd[:, None], "e4m3")
    return {
        "keys_words": keysp[0],
        "keys_scales": keysp[1],
        "notes": (n((D, U)) * 1.0 / np.sqrt(D) * fd[:, None]).astype(np.float32),
        "users2": (n((D, Z)) * 1.0 / np.sqrt(D) * fd[:, None]).astype(np.float32),
        "rowf": (np.random.uniform(0.02, 0.08, (I, 1)) * fi[:, None]).astype(np.float32),
        "vals": (n((E, T)) / ti).astype(np.float32),
        "offs": striped(idx),
        "offs2": striped(idx2),
        "offs3": striped(idx3),
    }


def reference(keys_words, keys_scales, notes, users2, rowf, vals, offs, offs2, offs3):
    idx = unstriped(offs)
    idx2 = unstriped(offs2)
    idx3 = unstriped(offs3)
    keysu = unpack_weight(keys_words, keys_scales, "e4m3")
    keysidxg = keysu[:, idx]
    notesidx2q = mxq(f64(notes)[:, idx2], 0, "e4m3")
    g1 = keysidxg.T @ notesidx2q
    users2idx3q = mxq(f64(users2)[:, idx3], 0, "e4m3")
    g2 = keysidxg.T @ users2idx3q
    g0 = np.maximum(g1, g2)
    gr1 = g0 * f64(rowf)
    vt1 = f64(vals)[:, idx].T
    vt1q = mxq(vt1, 0, "e4m3")
    gr1q = mxq(gr1, 0, "e4m3")
    o = vt1q.T @ gr1q
    return o

@@ -1,0 +1,169 @@
+from contextlib import ExitStack
+
+import concourse.mybir as mybir
+from concourse.masks import make_identity
+
+D, T, I, J, U, E = 512, 2048, 512, 512, 1024, 512
+FLOPS = 2 * (2 * D * I * J + I * E * J)
+
+F32 = mybir.dt.float32
+BF16 = mybir.dt.bfloat16
+I32 = mybir.dt.int32
+U32 = mybir.dt.uint32
+U16 = mybir.dt.uint16
+U8 = mybir.dt.uint8
+FP8X4 = mybir.dt.float8_e4m3fn_x4
+COPY = mybir.ActivationFunctionType.Copy
+MAX = mybir.AluOpType.max
+MULT = mybir.AluOpType.mult
+
+P = 128
+PACK = 4
+LIST_COLS = 32
+HALF = 256
+
+
+def tile_attend_tab_larger_exchange_kernel(tc, keys_words, keys_scales, notes, users2, rowf, vals, offs, offs2, offs3, out):
+    nc = tc.nc
+    with ExitStack() as ctx:
+        keep = ctx.enter_context(tc.tile_pool(name="keep", bufs=1))
+        psum = ctx.enter_context(tc.psum_pool(name="psum", bufs=1))
+
+        def sb(name, shape, dtype, tag=None):
+            return keep.tile(shape, dtype, name=name, tag=tag or name, align_bytes=64)
+
+        def gather(engine, dst, window, offsets):
+            if engine == "vector":
+                nc.vector.tensor_copy(dst, window[:].indirect(offsets))
+            else:
+                nc.scalar.activation(dst, window[:].indirect(offsets), COPY)
+
+        def interleave(dst, planes):
+            nc.vector.tensor_copy(
+                dst.rearrange("p (c i) t -> p c t i", i=4),
+                planes.rearrange("p t (c i) -> p c t i", i=4),
+            )
+
+        def quantise(codes, scales, values):
+            nc.vector.quantize_mx(out=codes.bitcast(FP8X4), scales=scales, in_=values.rearrange("p c t -> p (c t)"))
+
+        def product(acc, lhs, lhs_scales, rhs, rhs_scales):
+            nc.tensor.matmul_mx(out=acc, lhsT=lhs.bitcast(FP8X4), lhsT_scale=lhs_scales,
+                                rhs=rhs.bitcast(FP8X4), rhs_scale=rhs_scales, start=True, stop=True)
+
+        list_keys = sb("list_keys", [P, LIST_COLS], U16)
+        list_notes = sb("list_notes", [P, LIST_COLS], U16)
+        list_users = sb("list_users", [P, LIST_COLS], U16)
+        note_pool = [sb("note_pool%d" % t, [P, U], F32) for t in range(PACK)]
+        user_pool = [sb("user_pool%d" % t, [P, U], F32) for t in range(PACK)]
+        val_pool = [sb("val_pool%d" % b, [P, T], F32) for b in range(PACK)]
+        key_word_pool = sb("key_word_pool", [P, T], U32)
+        key_scale_pool = sb("key_scale_pool", [P, T], U8)
+        factor = sb("factor", [P, PACK], F32)
+        identity = sb("identity", [P, P], F32)
+
+        nc.vector.memset(key_scale_pool[:].bitcast(I32), 0)
+        notes_planes = notes.rearrange("(p t) u -> t p u", t=PACK)
+        users_planes = users2.rearrange("(p t) u -> t p u", t=PACK)
+        nc.sync.dma_start(list_notes[:], offs2)
+        for t in range(PACK):
+            nc.sync.dma_start(note_pool[t][:], notes_planes[t])
+            if t == 0:
+                nc.sync.dma_start(list_keys[:], offs)
+        for q in range(4):
+            nc.gpsimd.dma_start(key_scale_pool[32 * q : 32 * q + 4, :].bitcast(I32),
+                                keys_scales[0, 4 * q : 4 * q + 4, :].bitcast(I32))
+        nc.gpsimd.dma_start(factor[:], rowf.rearrange("(p t) o -> p (t o)", t=PACK))
+        nc.sync.dma_start(key_word_pool[:].bitcast(I32), keys_words[0].rearrange("p n t -> p (n t)").bitcast(I32))
+        nc.sync.dma_start(list_users[:], offs3)
+        for t in range(PACK):
+            nc.sync.dma_start(user_pool[t][:], users_planes[t])
+        for b in range(PACK):
+            nc.sync.dma_start(val_pool[b][:], vals[P * b : P * (b + 1), :])
+        make_identity(nc, identity[:])
+
+        note_planes = sb("note_planes", [P, PACK, J], BF16)
+        key_scales = sb("key_scales", [P, I], U8)
+        key_words = sb("key_words", [P, I], U32)
+        gather("vector", key_scales[:].rearrange("p (t s) -> p s t", t=PACK), key_scale_pool, list_keys[:])
+        for t in range(PACK):
+            gather("scalar" if t < PACK - 1 else "vector", note_planes[:, t, :], note_pool[t], list_notes[:])
+        note_bf = sb("note_bf", [P, J, PACK], BF16)
+        interleave(note_bf[:], note_planes[:])
+        gather("vector", key_words[:].rearrange("p (t s) -> p s t", t=PACK), key_word_pool, list_keys[:])
+        note_codes = sb("note_codes", [P, J], U32)
+        note_scales = sb("note_scales", [P, J], U8)
+        quantise(note_codes[:], note_scales[:], note_bf[:])
+
+        def table_chunk(codes, scales, cols):
+            acc = psum.tile([P, PACK, P], F32, name="acc", tag="acc", bufs=6)
+            for t in range(PACK):
+                rows = slice(P * t, P * (t + 1))
+                product(acc[:, t, :], key_words[:, rows], key_scales[:, rows], codes[:, cols], scales[:, cols])
+            return acc[:].rearrange("p t n -> p n t")
+
+        user_planes = [sb("user_planes%d" % h, [P, PACK, HALF], BF16) for h in range(2)]
+        half_list = [list_users[:, 16 * h : 16 * (h + 1)] for h in range(2)]
+        g1 = [sb("g1_%d" % c, [P, P, PACK], F32) for c in range(PACK)]
+        for t in range(PACK):
+            for h in range(2):
+                gather("scalar", user_planes[h][:, t, :], user_pool[t], half_list[h])
+        for c in range(PACK):
+            nc.vector.tensor_copy(g1[c][:], table_chunk(note_codes, note_scales, slice(P * c, P * (c + 1))))
+        user_bf = [sb("user_bf%d" % h, [P, HALF, PACK], BF16) for h in range(2)]
+        user_codes = [sb("user_codes%d" % h, [P, HALF], U32) for h in range(2)]
+        user_scales = [sb("user_scales%d" % h, [P, HALF], U8) for h in range(2)]
+        for h in range(2):
+            interleave(user_bf[h][:], user_planes[h][:])
+        for h in range(2):
+            quantise(user_codes[h][:], user_scales[h][:], user_bf[h][:])
+
+        larger = [sb("larger%d" % c, [P, P, PACK], F32) for c in range(PACK)]
+        table_bf = [sb("table_bf%d" % c, [P, P, PACK], BF16) for c in range(PACK)]
+        table_codes = sb("table_codes", [P, J], U32)
+        table_scales = sb("table_scales", [P, J], U8)
+        spread = factor[:].unsqueeze(1).to_broadcast([P, P, PACK])
+
+        def take_larger(c):
+            cols = slice(P * (c % 2), P * (c % 2 + 1))
+            nc.vector.tensor_tensor(larger[c][:], table_chunk(user_codes[c // 2], user_scales[c // 2], cols), g1[c][:], MAX)
+
+        def scale_rows(c):
+            nc.vector.tensor_tensor(table_bf[c][:], larger[c][:], spread, MULT)
+
+        def quantise_table(c):
+            cols = slice(P * c, P * (c + 1))
+            quantise(table_codes[:, cols], table_scales[:, cols], table_bf[c][:])
+
+        for step in range(PACK + 2):
+            if step < PACK:
+                take_larger(step)
+            if 1 <= step <= PACK:
+                scale_rows(step - 1)
+            if step >= 2:
+                quantise_table(step - 2)
+
+        val_codes = [sb("val_codes%d" % b, [P, P], U32, tag="table_bf%d" % min(b + 1, PACK - 1) if b < PACK - 1 else None) for b in range(PACK)]
+        val_scales = [sb("val_scales%d" % b, [P, P], U8) for b in range(PACK)]
+        for b in range(PACK):
+            picked = sb("picked", [P, I], BF16)
+            gather("scalar", picked[:], val_pool[b], list_keys[:])
+            words = picked[:].bitcast(F32)
+            turned = psum.tile([P, 2, P], F32, name="turned", tag="turned", bufs=2)
+            for u in range(2):
+                nc.tensor.transpose(turned[:, u, :], words[:, u::2], identity[:])
+            val_bf = sb("val_bf%d" % b, [P, P, PACK], BF16)
+            nc.scalar.copy(val_bf[:].bitcast(F32), turned[:].rearrange("p u e -> p e u"))
+            quantise(val_codes[b][:], val_scales[b][:], val_bf[:])
+
+        for b in range(PACK):
+            for h in range(2):
+                cols = slice(HALF * h, HALF * (h + 1))
+                acc = psum.tile([P, HALF], F32, name="acc", tag="acc", bufs=6)
+                product(acc[:], val_codes[b][:], val_scales[b][:], table_codes[:, cols], table_scales[:, cols])
+                result = sb("result%d_%d" % (b, h), [P, HALF], F32)
+                if h == 0:
+                    nc.vector.tensor_copy(result[:], acc[:])
+                else:
+                    nc.scalar.copy(result[:], acc[:])
+                nc.sync.dma_start(out[P * b : P * (b + 1), cols], result[:])

@@ -27,6 +27,7 @@ def tile_attend_tab_larger_exchange_kernel(tc, keys_words, keys_scales, notes, u
     nc = tc.nc
     with ExitStack() as ctx:
         keep = ctx.enter_context(tc.tile_pool(name="keep", bufs=1))
+        shared = ctx.enter_context(tc.tile_pool(name="shared", bufs=1))
         psum = ctx.enter_context(tc.psum_pool(name="psum", bufs=1))
 
         def sb(name, shape, dtype, tag=None):
@@ -38,8 +39,8 @@ def tile_attend_tab_larger_exchange_kernel(tc, keys_words, keys_scales, notes, u
             else:
                 nc.scalar.activation(dst, window[:].indirect(offsets), COPY)
 
-        def interleave(dst, planes):
-            nc.vector.tensor_copy(
+        def interleave(engine, dst, planes):
+            (nc.vector.tensor_copy if engine == "vector" else nc.scalar.copy)(
                 dst.rearrange("p (c i) t -> p c t i", i=4),
                 planes.rearrange("p t (c i) -> p c t i", i=4),
             )
@@ -56,67 +57,86 @@ def tile_attend_tab_larger_exchange_kernel(tc, keys_words, keys_scales, notes, u
         list_users = sb("list_users", [P, LIST_COLS], U16)
         note_pool = [sb("note_pool%d" % t, [P, U], F32) for t in range(PACK)]
         user_pool = [sb("user_pool%d" % t, [P, U], F32) for t in range(PACK)]
-        val_pool = [sb("val_pool%d" % b, [P, T], F32) for b in range(PACK)]
+        val_pool = [sb("val_pool%d" % b, [P, T], F32) for b in range(PACK - 1)]
+        val_pool.append(shared.tile([P, T], F32, name="val_pool3", offset=0, align_bytes=64))
         key_word_pool = sb("key_word_pool", [P, T], U32)
         key_scale_pool = sb("key_scale_pool", [P, T], U8)
         factor = sb("factor", [P, PACK], F32)
         identity = sb("identity", [P, P], F32)
 
-        nc.vector.memset(key_scale_pool[:].bitcast(I32), 0)
+        nc.gpsimd.memset(key_scale_pool[:].bitcast(I32), 0)
         notes_planes = notes.rearrange("(p t) u -> t p u", t=PACK)
         users_planes = users2.rearrange("(p t) u -> t p u", t=PACK)
         nc.sync.dma_start(list_notes[:], offs2)
         for t in range(PACK):
             nc.sync.dma_start(note_pool[t][:], notes_planes[t])
             if t == 0:
+                for q in range(4):
+                    nc.sync.dma_start(key_scale_pool[32 * q : 32 * q + 4, :].bitcast(I32),
+                                      keys_scales[0, 4 * q : 4 * q + 4, :].bitcast(I32))
                 nc.sync.dma_start(list_keys[:], offs)
-        for q in range(4):
-            nc.gpsimd.dma_start(key_scale_pool[32 * q : 32 * q + 4, :].bitcast(I32),
-                                keys_scales[0, 4 * q : 4 * q + 4, :].bitcast(I32))
-        nc.gpsimd.dma_start(factor[:], rowf.rearrange("(p t) o -> p (t o)", t=PACK))
         nc.sync.dma_start(key_word_pool[:].bitcast(I32), keys_words[0].rearrange("p n t -> p (n t)").bitcast(I32))
         nc.sync.dma_start(list_users[:], offs3)
+        nc.sync.dma_start(factor[:], rowf.rearrange("(p t) o -> p (t o)", t=PACK))
         for t in range(PACK):
             nc.sync.dma_start(user_pool[t][:], users_planes[t])
         for b in range(PACK):
             nc.sync.dma_start(val_pool[b][:], vals[P * b : P * (b + 1), :])
         make_identity(nc, identity[:])
 
-        note_planes = sb("note_planes", [P, PACK, J], BF16)
+        def halves(name, shape, dtype):
+            return [sb("%s%d" % (name, h), shape, dtype) for h in range(2)]
+
         key_scales = sb("key_scales", [P, I], U8)
         key_words = sb("key_words", [P, I], U32)
         gather("vector", key_scales[:].rearrange("p (t s) -> p s t", t=PACK), key_scale_pool, list_keys[:])
-        for t in range(PACK):
-            gather("scalar" if t < PACK - 1 else "vector", note_planes[:, t, :], note_pool[t], list_notes[:])
-        note_bf = sb("note_bf", [P, J, PACK], BF16)
-        interleave(note_bf[:], note_planes[:])
-        gather("vector", key_words[:].rearrange("p (t s) -> p s t", t=PACK), key_word_pool, list_keys[:])
-        note_codes = sb("note_codes", [P, J], U32)
-        note_scales = sb("note_scales", [P, J], U8)
-        quantise(note_codes[:], note_scales[:], note_bf[:])
 
-        def table_chunk(codes, scales, cols):
-            acc = psum.tile([P, PACK, P], F32, name="acc", tag="acc", bufs=6)
+        def gather_planes(planes, pool, whole_list, engines):
+            for t in range(PACK):
+                for h in range(2):
+                    gather(engines[t][h], planes[h][:, t, :], pool[t], whole_list[:, 16 * h : 16 * (h + 1)])
+
+        def lay_out(name, engine, planes):
+            bf = sb(name + "_bf", [P, planes.shape[2], PACK], BF16)
+            interleave(engine, bf[:], planes)
+            return bf
+
+        def quantise_columns(name, bf, tag=None):
+            width = bf.shape[1]
+            codes = sb(name + "_codes", [P, width], U32, tag=tag)
+            scales = sb(name + "_scales", [P, width], U8)
+            quantise(codes[:], scales[:], bf[:])
+            return [(codes[:, first : first + P], scales[:, first : first + P]) for first in range(0, width, P)]
+
+        S, V = "scalar", "vector"
+        note_planes = halves("note_planes", [P, PACK, HALF], BF16)
+        gather_planes(note_planes, note_pool, list_notes, [(S, S), (S, S), (S, S), (V, S)])
+        note_bf = [lay_out("note%d" % h, (V, S)[h], note_planes[h][:]) for h in range(2)]
+        note_mx = quantise_columns("note0", note_bf[0])
+        gather("vector", key_words[:].rearrange("p (t s) -> p s t", t=PACK), key_word_pool, list_keys[:])
+        note_mx.extend(quantise_columns("note1", note_bf[1], tag="key_word_pool"))
+
+        def bank(n, shape):
+            return psum.tile(shape, F32, name="bank%d" % n)
+
+        def table_chunk(operand, c, first_bank):
+            codes, scales = operand[c]
+            acc = bank(first_bank + c, [P, PACK, P])
             for t in range(PACK):
                 rows = slice(P * t, P * (t + 1))
-                product(acc[:, t, :], key_words[:, rows], key_scales[:, rows], codes[:, cols], scales[:, cols])
+                product(acc[:, t, :], key_words[:, rows], key_scales[:, rows], codes, scales)
             return acc[:].rearrange("p t n -> p n t")
 
-        user_planes = [sb("user_planes%d" % h, [P, PACK, HALF], BF16) for h in range(2)]
-        half_list = [list_users[:, 16 * h : 16 * (h + 1)] for h in range(2)]
+        user_planes = halves("user_planes", [P, PACK, HALF], BF16)
         g1 = [sb("g1_%d" % c, [P, P, PACK], F32) for c in range(PACK)]
-        for t in range(PACK):
-            for h in range(2):
-                gather("scalar", user_planes[h][:, t, :], user_pool[t], half_list[h])
         for c in range(PACK):
-            nc.vector.tensor_copy(g1[c][:], table_chunk(note_codes, note_scales, slice(P * c, P * (c + 1))))
-        user_bf = [sb("user_bf%d" % h, [P, HALF, PACK], BF16) for h in range(2)]
-        user_codes = [sb("user_codes%d" % h, [P, HALF], U32) for h in range(2)]
-        user_scales = [sb("user_scales%d" % h, [P, HALF], U8) for h in range(2)]
-        for h in range(2):
-            interleave(user_bf[h][:], user_planes[h][:])
-        for h in range(2):
-            quantise(user_codes[h][:], user_scales[h][:], user_bf[h][:])
+            nc.vector.tensor_copy(g1[c][:], table_chunk(note_mx, c, 0))
+        gather_planes(user_planes, user_pool, list_users, [(S, S), (S, S), (S, S), (V, S)])
+        user_bf = [lay_out("user%d" % c, V, user_planes[0][:, :, P * c : P * (c + 1)]) for c in range(2)]
+        user_bf.append(lay_out("user2", S, user_planes[1][:]))
+        user_mx = []
+        for n in range(2):
+            user_mx.extend(quantise_columns("user%d" % n, user_bf[n]))
 
         larger = [sb("larger%d" % c, [P, P, PACK], F32) for c in range(PACK)]
         table_bf = [sb("table_bf%d" % c, [P, P, PACK], BF16) for c in range(PACK)]
@@ -125,8 +145,7 @@ def tile_attend_tab_larger_exchange_kernel(tc, keys_words, keys_scales, notes, u
         spread = factor[:].unsqueeze(1).to_broadcast([P, P, PACK])
 
         def take_larger(c):
-            cols = slice(P * (c % 2), P * (c % 2 + 1))
-            nc.vector.tensor_tensor(larger[c][:], table_chunk(user_codes[c // 2], user_scales[c // 2], cols), g1[c][:], MAX)
+            nc.vector.tensor_tensor(larger[c][:], table_chunk(user_mx, c, PACK), g1[c][:], MAX)
 
         def scale_rows(c):
             nc.vector.tensor_tensor(table_bf[c][:], larger[c][:], spread, MULT)
@@ -138,32 +157,54 @@ def tile_attend_tab_larger_exchange_kernel(tc, keys_words, keys_scales, notes, u
         for step in range(PACK + 2):
             if step < PACK:
                 take_larger(step)
+            if step == 0:
+                user_mx.extend(quantise_columns("user2", user_bf[2], tag="g1_0"))
             if 1 <= step <= PACK:
                 scale_rows(step - 1)
             if step >= 2:
                 quantise_table(step - 2)
 
-        val_codes = [sb("val_codes%d" % b, [P, P], U32, tag="table_bf%d" % min(b + 1, PACK - 1) if b < PACK - 1 else None) for b in range(PACK)]
-        val_scales = [sb("val_scales%d" % b, [P, P], U8) for b in range(PACK)]
-        for b in range(PACK):
-            picked = sb("picked", [P, I], BF16)
-            gather("scalar", picked[:], val_pool[b], list_keys[:])
+        pair_bf = sb("pair_bf", [P, 2 * P, PACK], BF16, tag="val_pool1")
+        pair_scales = sb("pair_scales", [P, 2 * P], U8)
+        val_bf = [pair_bf[:, :P, :], pair_bf[:, P:, :]] + [sb("val_bf%d" % b, [P, P, PACK], BF16)[:] for b in (2, 3)]
+        val_scales = [pair_scales[:, :P], pair_scales[:, P:]] + [sb("val_scales%d" % b, [P, P], U8)[:] for b in (2, 3)]
+
+        def turn(b):
+            picked = sb("picked%d" % b, [P, I], BF16)
+            if b < PACK - 1:
+                gather(S, picked[:], val_pool[b], list_keys[:])
+            else:
+                gather(V, picked[:, :HALF], val_pool[b], list_keys[:, :16])
+                gather(S, picked[:, HALF:], val_pool[b], list_keys[:, 16:])
             words = picked[:].bitcast(F32)
-            turned = psum.tile([P, 2, P], F32, name="turned", tag="turned", bufs=2)
+            turned = bank(PACK + b, [P, 2, P])
             for u in range(2):
                 nc.tensor.transpose(turned[:, u, :], words[:, u::2], identity[:])
-            val_bf = sb("val_bf%d" % b, [P, P, PACK], BF16)
-            nc.scalar.copy(val_bf[:].bitcast(F32), turned[:].rearrange("p u e -> p e u"))
-            quantise(val_codes[b][:], val_scales[b][:], val_bf[:])
+            nc.scalar.copy(val_bf[b].bitcast(F32), turned[:].rearrange("p u e -> p e u"))
 
-        for b in range(PACK):
-            for h in range(2):
-                cols = slice(HALF * h, HALF * (h + 1))
-                acc = psum.tile([P, HALF], F32, name="acc", tag="acc", bufs=6)
-                product(acc[:], val_codes[b][:], val_scales[b][:], table_codes[:, cols], table_scales[:, cols])
-                result = sb("result%d_%d" % (b, h), [P, HALF], F32)
-                if h == 0:
-                    nc.vector.tensor_copy(result[:], acc[:])
-                else:
-                    nc.scalar.copy(result[:], acc[:])
-                nc.sync.dma_start(out[P * b : P * (b + 1), cols], result[:])
+        turn(0)
+        turn(1)
+        turn(2)
+        pair_codes = sb("pair_codes", [P, 2 * P], U32, tag="val_pool2")
+        val_codes = [pair_codes[:, :P], pair_codes[:, P:]]
+        quantise(pair_codes[:], pair_scales[:], pair_bf[:])
+        turn(3)
+        val_codes.append(shared.tile([P, P], U32, name="val_codes2", offset=2 * J * 4, align_bytes=64)[:])
+        val_codes.append(sb("val_codes3", [P, P], U32)[:])
+        for b in (2, 3):
+            quantise(val_codes[b], val_scales[b], val_bf[b])
+
+        pieces = [(0, 0, J, V), (1, 0, J, S), (2, 0, J, S), (3, 0, HALF, V), (3, HALF, J, S)]
+        for n, (b, first, last, engine) in enumerate(pieces):
+            cols = slice(first, last)
+            acc = bank(n, [P, last - first])
+            product(acc[:], val_codes[b], val_scales[b], table_codes[:, cols], table_scales[:, cols])
+            if n < 2:
+                result = shared.tile([P, J], F32, name="result%d" % n, offset=n * J * 4, align_bytes=64)
+            else:
+                result = sb("result%d" % n, [P, last - first], F32)
+            if engine == V:
+                nc.vector.tensor_copy(result[:], acc[:])
+            else:
+                nc.scalar.copy(result[:], acc[:])
+            nc.sync.dma_start(out[P * b : P * (b + 1), cols], result[:])

from contextlib import ExitStack

import concourse.mybir as mybir
from concourse.masks import make_identity

D, T, I, J, U, E = 512, 2048, 512, 512, 1024, 512
FLOPS = 2 * (2 * D * I * J + I * E * J)

F32 = mybir.dt.float32
BF16 = mybir.dt.bfloat16
I32 = mybir.dt.int32
U32 = mybir.dt.uint32
U16 = mybir.dt.uint16
U8 = mybir.dt.uint8
FP8X4 = mybir.dt.float8_e4m3fn_x4
COPY = mybir.ActivationFunctionType.Copy
MAX = mybir.AluOpType.max
MULT = mybir.AluOpType.mult

P = 128
PACK = 4
LIST_COLS = 32
HALF = 256


def tile_attend_tab_larger_exchange_kernel(tc, keys_words, keys_scales, notes, users2, rowf, vals, offs, offs2, offs3, out):
    nc = tc.nc
    with ExitStack() as ctx:
        keep = ctx.enter_context(tc.tile_pool(name="keep", bufs=1))
        shared = ctx.enter_context(tc.tile_pool(name="shared", bufs=1))
        psum = ctx.enter_context(tc.psum_pool(name="psum", bufs=1))

        def sb(name, shape, dtype, tag=None):
            return keep.tile(shape, dtype, name=name, tag=tag or name, align_bytes=64)

        def gather(engine, dst, window, offsets):
            if engine == "vector":
                nc.vector.tensor_copy(dst, window[:].indirect(offsets))
            else:
                nc.scalar.activation(dst, window[:].indirect(offsets), COPY)

        def interleave(engine, dst, planes):
            (nc.vector.tensor_copy if engine == "vector" else nc.scalar.copy)(
                dst.rearrange("p (c i) t -> p c t i", i=4),
                planes.rearrange("p t (c i) -> p c t i", i=4),
            )

        def quantise(codes, scales, values):
            nc.vector.quantize_mx(out=codes.bitcast(FP8X4), scales=scales, in_=values.rearrange("p c t -> p (c t)"))

        def product(acc, lhs, lhs_scales, rhs, rhs_scales):
            nc.tensor.matmul_mx(out=acc, lhsT=lhs.bitcast(FP8X4), lhsT_scale=lhs_scales,
                                rhs=rhs.bitcast(FP8X4), rhs_scale=rhs_scales, start=True, stop=True)

        list_keys = sb("list_keys", [P, LIST_COLS], U16)
        list_notes = sb("list_notes", [P, LIST_COLS], U16)
        list_users = sb("list_users", [P, LIST_COLS], U16)
        note_pool = [sb("note_pool%d" % t, [P, U], F32) for t in range(PACK)]
        user_pool = [sb("user_pool%d" % t, [P, U], F32) for t in range(PACK)]
        val_pool = [sb("val_pool%d" % b, [P, T], F32) for b in range(PACK - 1)]
        val_pool.append(shared.tile([P, T], F32, name="val_pool3", offset=0, align_bytes=64))
        key_word_pool = sb("key_word_pool", [P, T], U32)
        key_scale_pool = sb("key_scale_pool", [P, T], U8)
        factor = sb("factor", [P, PACK], F32)
        identity = sb("identity", [P, P], F32)

        nc.gpsimd.memset(key_scale_pool[:].bitcast(I32), 0)
        notes_planes = notes.rearrange("(p t) u -> t p u", t=PACK)
        users_planes = users2.rearrange("(p t) u -> t p u", t=PACK)
        nc.sync.dma_start(list_notes[:], offs2)
        for t in range(PACK):
            nc.sync.dma_start(note_pool[t][:], notes_planes[t])
            if t == 0:
                for q in range(4):
                    nc.sync.dma_start(key_scale_pool[32 * q : 32 * q + 4, :].bitcast(I32),
                                      keys_scales[0, 4 * q : 4 * q + 4, :].bitcast(I32))
                nc.sync.dma_start(list_keys[:], offs)
        nc.sync.dma_start(key_word_pool[:].bitcast(I32), keys_words[0].rearrange("p n t -> p (n t)").bitcast(I32))
        nc.sync.dma_start(list_users[:], offs3)
        nc.sync.dma_start(factor[:], rowf.rearrange("(p t) o -> p (t o)", t=PACK))
        for t in range(PACK):
            nc.sync.dma_start(user_pool[t][:], users_planes[t])
        for b in range(PACK):
            nc.sync.dma_start(val_pool[b][:], vals[P * b : P * (b + 1), :])
        make_identity(nc, identity[:])

        def halves(name, shape, dtype):
            return [sb("%s%d" % (name, h), shape, dtype) for h in range(2)]

        key_scales = sb("key_scales", [P, I], U8)
        key_words = sb("key_words", [P, I], U32)
        gather("vector", key_scales[:].rearrange("p (t s) -> p s t", t=PACK), key_scale_pool, list_keys[:])

        def gather_planes(planes, pool, whole_list, engines):
            for t in range(PACK):
                for h in range(2):
                    gather(engines[t][h], planes[h][:, t, :], pool[t], whole_list[:, 16 * h : 16 * (h + 1)])

        def lay_out(name, engine, planes):
            bf = sb(name + "_bf", [P, planes.shape[2], PACK], BF16)
            interleave(engine, bf[:], planes)
            return bf

        def quantise_columns(name, bf, tag=None):
            width = bf.shape[1]
            codes = sb(name + "_codes", [P, width], U32, tag=tag)
            scales = sb(name + "_scales", [P, width], U8)
            quantise(codes[:], scales[:], bf[:])
            return [(codes[:, first : first + P], scales[:, first : first + P]) for first in range(0, width, P)]

        S, V = "scalar", "vector"
        note_planes = halves("note_planes", [P, PACK, HALF], BF16)
        gather_planes(note_planes, note_pool, list_notes, [(S, S), (S, S), (S, S), (V, S)])
        note_bf = [lay_out("note%d" % h, (V, S)[h], note_planes[h][:]) for h in range(2)]
        note_mx = quantise_columns("note0", note_bf[0])
        gather("vector", key_words[:].rearrange("p (t s) -> p s t", t=PACK), key_word_pool, list_keys[:])
        note_mx.extend(quantise_columns("note1", note_bf[1], tag="key_word_pool"))

        def bank(n, shape):
            return psum.tile(shape, F32, name="bank%d" % n)

        def table_chunk(operand, c, first_bank):
            codes, scales = operand[c]
            acc = bank(first_bank + c, [P, PACK, P])
            for t in range(PACK):
                rows = slice(P * t, P * (t + 1))
                product(acc[:, t, :], key_words[:, rows], key_scales[:, rows], codes, scales)
            return acc[:].rearrange("p t n -> p n t")

        user_planes = halves("user_planes", [P, PACK, HALF], BF16)
        g1 = [sb("g1_%d" % c, [P, P, PACK], F32) for c in range(PACK)]
        for c in range(PACK):
            nc.vector.tensor_copy(g1[c][:], table_chunk(note_mx, c, 0))
        gather_planes(user_planes, user_pool, list_users, [(S, S), (S, S), (S, S), (V, S)])
        user_bf = [lay_out("user%d" % c, V, user_planes[0][:, :, P * c : P * (c + 1)]) for c in range(2)]
        user_bf.append(lay_out("user2", S, user_planes[1][:]))
        user_mx = []
        for n in range(2):
            user_mx.extend(quantise_columns("user%d" % n, user_bf[n]))

        larger = [sb("larger%d" % c, [P, P, PACK], F32) for c in range(PACK)]
        table_bf = [sb("table_bf%d" % c, [P, P, PACK], BF16) for c in range(PACK)]
        table_codes = sb("table_codes", [P, J], U32)
        table_scales = sb("table_scales", [P, J], U8)
        spread = factor[:].unsqueeze(1).to_broadcast([P, P, PACK])

        def take_larger(c):
            nc.vector.tensor_tensor(larger[c][:], table_chunk(user_mx, c, PACK), g1[c][:], MAX)

        def scale_rows(c):
            nc.vector.tensor_tensor(table_bf[c][:], larger[c][:], spread, MULT)

        def quantise_table(c):
            cols = slice(P * c, P * (c + 1))
            quantise(table_codes[:, cols], table_scales[:, cols], table_bf[c][:])

        for step in range(PACK + 2):
            if step < PACK:
                take_larger(step)
            if step == 0:
                user_mx.extend(quantise_columns("user2", user_bf[2], tag="g1_0"))
            if 1 <= step <= PACK:
                scale_rows(step - 1)
            if step >= 2:
                quantise_table(step - 2)

        pair_bf = sb("pair_bf", [P, 2 * P, PACK], BF16, tag="val_pool1")
        pair_scales = sb("pair_scales", [P, 2 * P], U8)
        val_bf = [pair_bf[:, :P, :], pair_bf[:, P:, :]] + [sb("val_bf%d" % b, [P, P, PACK], BF16)[:] for b in (2, 3)]
        val_scales = [pair_scales[:, :P], pair_scales[:, P:]] + [sb("val_scales%d" % b, [P, P], U8)[:] for b in (2, 3)]

        def turn(b):
            picked = sb("picked%d" % b, [P, I], BF16)
            if b < PACK - 1:
                gather(S, picked[:], val_pool[b], list_keys[:])
            else:
                gather(V, picked[:, :HALF], val_pool[b], list_keys[:, :16])
                gather(S, picked[:, HALF:], val_pool[b], list_keys[:, 16:])
            words = picked[:].bitcast(F32)
            turned = bank(PACK + b, [P, 2, P])
            for u in range(2):
                nc.tensor.transpose(turned[:, u, :], words[:, u::2], identity[:])
            nc.scalar.copy(val_bf[b].bitcast(F32), turned[:].rearrange("p u e -> p e u"))

        turn(0)
        turn(1)
        turn(2)
        pair_codes = sb("pair_codes", [P, 2 * P], U32, tag="val_pool2")
        val_codes = [pair_codes[:, :P], pair_codes[:, P:]]
        quantise(pair_codes[:], pair_scales[:], pair_bf[:])
        turn(3)
        val_codes.append(shared.tile([P, P], U32, name="val_codes2", offset=2 * J * 4, align_bytes=64)[:])
        val_codes.append(sb("val_codes3", [P, P], U32)[:])
        for b in (2, 3):
            quantise(val_codes[b], val_scales[b], val_bf[b])

        pieces = [(0, 0, J, V), (1, 0, J, S), (2, 0, J, S), (3, 0, HALF, V), (3, HALF, J, S)]
        for n, (b, first, last, engine) in enumerate(pieces):
            cols = slice(first, last)
            acc = bank(n, [P, last - first])
            product(acc[:], val_codes[b], val_scales[b], table_codes[:, cols], table_scales[:, cols])
            if n < 2:
                result = shared.tile([P, J], F32, name="result%d" % n, offset=n * J * 4, align_bytes=64)
            else:
                result = sb("result%d" % n, [P, last - first], F32)
            if engine == V:
                nc.vector.tensor_copy(result[:], acc[:])
            else:
                nc.scalar.copy(result[:], acc[:])
            nc.sync.dma_start(out[P * b : P * (b + 1), cols], result[:])
